import numpy as np
import ml_dtypes


def mxq(x, axis, fmt="e4m3"):
    dtype, down = {"e4m3": (ml_dtypes.float8_e4m3fn, 7), "e5m2": (ml_dtypes.float8_e5m2, 14)}[fmt]
    v = np.moveaxis(np.asarray(x, np.float32).astype(ml_dtypes.bfloat16).astype(np.float64), axis, -1)
    blocks = v.reshape(v.shape[:-1] + (-1, 32))
    amax = np.abs(blocks).max(-1, keepdims=True)
    byte = np.maximum(np.where(amax > 0, np.frexp(amax)[1] - 1 + 127, 0) - down, 1)
    scale = np.exp2(byte - 127.0)
    codes = (blocks / scale).astype(np.float32).astype(dtype).astype(np.float64)
    return np.moveaxis((codes * scale).reshape(v.shape), -1, axis)


WIDE = False


def mx_kscale(k):
    if not WIDE:
        return np.ones(k)
    levels = np.array([10, -10, 5, -5, 0])
    if k % 512:
        return np.exp2(np.random.permutation(np.resize(levels, k // 32))).repeat(32)
    a = np.empty((k // 512, 16))
    for p in range(k // 512):
        a[p, :8] = np.random.permutation(np.resize(levels, 8))
        for g in range(8):
            far = levels[np.abs(levels - a[p, g]) >= 10]
            a[p, g + 8] = far[np.random.randint(len(far))]
    return np.exp2(a.ravel()).repeat(32)


BF16 = ml_dtypes.bfloat16


def bf(x):
    return np.asarray(x, np.float32).astype(BF16)


def f64(x):
    return np.asarray(x).astype(np.float64)


E2M1 = np.array([0.0, 0.5, 1.0, 1.5, 2.0, 3.0, 4.0, 6.0, -0.0, -0.5, -1.0, -1.5, -2.0, -3.0, -4.0, -6.0])


def pack_weight(w, fmt):
    k, n = w.shape
    w = f64(bf(w)).reshape(k // 32, 32, n)
    amax = np.abs(w).max(1)
    if fmt == "e4m3":
        byte = np.frexp(amax)[1] - 1 + 127 - 7
    else:
        mant, ex = np.frexp(amax / 6.0)
        byte = np.where(mant > 0.5, ex, ex - 1) + 127
    byte = np.clip(np.where(amax > 0, byte, 1), 1, 254)
    scaled = (w * np.exp2(127.0 - byte)[:, None, :]).reshape(k, n).astype(np.float32)
    by_word = np.ascontiguousarray(scaled.reshape(k // 512, 128, 4, n).transpose(0, 1, 3, 2))
    if fmt == "e4m3":
        words = by_word.astype(ml_dtypes.float8_e4m3fn).view(np.uint8)
    else:
        c = by_word.astype(ml_dtypes.float4_e2m1fn).view(np.uint8) & 0xF
        words = c[..., 0::2] | (c[..., 1::2] << 4)
    return np.ascontiguousarray(words), np.ascontiguousarray(byte.astype(np.uint8).reshape(k // 512, 16, n))


def unpack_weight(words, scales, fmt):
    g, p, n, _ = words.shape
    if fmt == "e4m3":
        vals = np.ascontiguousarray(words).view(ml_dtypes.float8_e4m3fn).astype(np.float64)
    else:
        nib = np.empty((g, p, n, 4), np.uint8)
        nib[..., 0::2] = words & 0xF
        nib[..., 1::2] = words >> 4
        vals = E2M1[nib]
    vals = vals * np.repeat(np.exp2(scales.astype(np.float64) - 127.0), 8, axis=1)[..., None]
    return vals.transpose(0, 1, 3, 2).reshape(g * 512, n)

def planes(Y):
    n, m = Y.shape
    b = f64(bf(Y)).reshape(n // 32, 32, m)
    amax = np.abs(b).max(1)
    byte = np.clip(np.where(amax > 0, np.frexp(amax)[1] - 1 + 127 - 7, 1), 1, 254)
    codes = (b * np.exp2(127.0 - byte)[:, None, :]).reshape(n, m).astype(np.float32).astype(ml_dtypes.float8_e4m3fn).view(np.uint8)
    words = codes.reshape(n // 512, 128, 4, m).transpose(0, 1, 3, 2)
    return np.ascontiguousarray(words), np.ascontiguousarray(byte.astype(np.uint8).reshape(n // 512, 16, m))


N, D, F = 2048, 512, 1024


def _remove_frame_mean(f):
    n_frames = f.shape[0]
    mean = np.sum(f, axis=0, keepdims=True) / n_frames
    return f - mean


def setup_inputs():
    s0, s1 = mx_kscale(D), mx_kscale(D)
    u = mx_kscale(N)
    x0 = bf(np.random.standard_normal((N, D)) * s0)
    x1 = bf(np.random.standard_normal((N, D)) * s1 / u[:, None])
    w0_words, w0_scales = pack_weight(np.random.standard_normal((D, F)) / np.sqrt(D) / s0[:, None], "e4m3")
    b = bf(np.random.standard_normal(F) * 0.5)
    w1_words, w1_scales = pack_weight(np.random.standard_normal((D, F)) / np.sqrt(D) / s1[:, None], "e4m3")
    fw = bf((1.0 + 0.3 * np.random.standard_normal(N)) * u)
    return {"x0": x0,
            "x1": x1,
            "w0_words": w0_words,
            "w0_scales": w0_scales,
            "b": b,
            "w1_words": w1_words,
            "w1_scales": w1_scales,
            "fw": fw}


def core(x0, x1, w0_words, w0_scales, b, w1_words, w1_scales, fw):
    n_frames = x0.shape[0]
    f = np.tanh((mxq(f64(x0), 1, "e4m3") @ unpack_weight(w0_words, w0_scales, "e4m3")) + f64(b)[None, :])
    fc = _remove_frame_mean(f)
    p = fc * f64(fw)[:, None]
    v = mxq(f64(x1), 1, "e4m3") @ unpack_weight(w1_words, w1_scales, "e4m3")
    c = (mxq(p, 0, "e4m3").T @ mxq(v, 0, "e4m3")) / np.sqrt(n_frames)
    return 0.5 * (c + c.T)


def reference(x0, x1, w0_words, w0_scales, b, w1_words, w1_scales, fw):
    R_out = core(x0, x1, w0_words, w0_scales, b, w1_words, w1_scales, fw)
    words, scales = planes(R_out.T)
    return R_out, words, scales

@@ -1,0 +1,411 @@
+import math
+from contextlib import ExitStack
+
+import concourse.mybir as mybir
+from concourse.masks import make_identity
+
+N, D, F = 2048, 512, 1024
+FLOPS = 2 * N * D * F * 2 + 2 * N * F * F
+
+F32 = mybir.dt.float32
+BF16 = mybir.dt.bfloat16
+U32 = mybir.dt.uint32
+I32 = mybir.dt.int32
+U8 = mybir.dt.uint8
+FP8X4 = mybir.dt.float8_e4m3fn_x4
+ACT = mybir.ActivationFunctionType
+ALU = mybir.AluOpType
+
+P = 128
+PASS = 512
+NG = N // PASS
+NT = F // P
+BANK = 512
+R_SCALE = 0.5 / math.sqrt(N)
+SB = 6
+VB = 0
+XS = 4
+A1 = 0.3
+
+
+def tile_symmetrisedweightedcrossmoment_kernel(
+    tc, x0, x1, w0_words, w0_scales, b, w1_words, w1_scales, fw, out_0, out_1, out_2
+):
+    nc = tc.nc
+    with ExitStack() as ctx:
+        keep = ctx.enter_context(tc.tile_pool(name="keep", bufs=1))
+        work = ctx.enter_context(tc.tile_pool(name="work", bufs=2))
+        psum = ctx.enter_context(tc.psum_pool(name="psum", bufs=1))
+        ctx.enter_context(tc.manual_schedule())
+
+        def bank(reader, shape, dtype=F32):
+            if VB == 0 or reader is nc.scalar:
+                return psum.tile(shape, dtype, name="sbank", tag="sbank", bufs=SB)
+            return psum.tile(shape, dtype, name="vbank", tag="vbank", bufs=VB)
+
+        def move(eng, out, in_):
+            if eng is nc.scalar:
+                eng.copy(out=out, in_=in_)
+            else:
+                eng.tensor_copy(out=out, in_=in_)
+
+        def mx(name, width):
+            codes = keep.tile([P, width], U32, name=name + "_codes", align_bytes=64)
+            scales = keep.tile([P, width], U8, name=name + "_scales", align_bytes=64)
+            return codes, scales
+
+        def quantise(dst, cols, src):
+            nc.vector.quantize_mx(out=dst[0][:, cols].bitcast(FP8X4), scales=dst[1][:, cols], in_=src)
+
+        def mx_pass(out, stat, stat_cols, mov, mov_cols, start, stop):
+            nc.tensor.matmul_mx(
+                out=out,
+                lhsT=stat[0][:, stat_cols].bitcast(FP8X4),
+                lhsT_scale=stat[1][:, stat_cols],
+                rhs=mov[0][:, mov_cols].bitcast(FP8X4),
+                rhs_scale=mov[1][:, mov_cols],
+                start=start,
+                stop=stop,
+            )
+
+        def feat(j):
+            return slice(j * P, (j + 1) * P)
+
+        ident = keep.tile([P, P], F32, name="ident")
+        ident_bf = keep.tile([P, P], BF16, name="ident_bf")
+        b_rows = keep.tile([P, P], BF16, name="b_rows")
+        b_col = keep.tile([P, NT], F32, name="b_col")
+        fw_rows = keep.tile([P, NG, 4], BF16, name="fw_rows")
+        fw_all = keep.tile([P, N], BF16, name="fw_all")
+        sums = keep.tile([P, NT * NG], F32, name="sums")
+        parts = keep.tile([P, NT * NG], F32, name="parts")
+        mean = keep.tile([P, NT], F32, name="mean")
+        warm = keep.tile([P, 8], F32, name="warm")
+        w0 = mx("w0", F)
+        w1 = mx("w1", F)
+        xq = [[mx("x%d_%d" % (s, g), PASS) for g in range(NG)] for s in range(2)]
+        pq = [mx("p%d" % g, F) for g in range(NG)]
+        vq = [mx("v%d" % g, F) for g in range(NG)]
+        x_raw = [[keep.tile([P, 4, D], BF16, name="xraw%d_%d" % (s, g)) for g in range(NG)] for s in range(2)]
+        r_bf = [keep.tile([P, NT, PASS], BF16, name="rbf%d" % g) for g in range(2)]
+        out_codes = [keep.tile([P, F], U32, name="ocodes%d" % g, align_bytes=64) for g in range(2)]
+        out_scales = keep.tile([P, F], U8, name="oscales", align_bytes=64)
+
+        def load_x(s, g):
+            src = (x0, x1)[s][g * PASS:(g + 1) * PASS, :]
+            nc.sync.dma_start(out=x_raw[s][g][:], in_=src.rearrange("(p t) d -> p t d", t=4))
+
+        def load_codes(w, words):
+            nc.sync.dma_start(out=w[0][:].bitcast(I32), in_=words[0].rearrange("p n t -> p (n t)").bitcast(I32))
+
+        def load_scales(queue, w, scales):
+            for q in range(4):
+                queue.dma_start(out=w[1][32 * q:32 * q + 4, :].bitcast(I32), in_=scales[0, 4 * q:4 * q + 4, :].bitcast(I32))
+
+        nc.vector.memset(w0[1][:].bitcast(I32), 0)
+        nc.vector.memset(w1[1][:].bitcast(I32), 0)
+        nc.vector.memset(b_rows[:], 0.0)
+        nc.vector.memset(warm[:], 0.0)
+        make_identity(nc, ident[:])
+        load_x(0, 0)
+        load_scales(nc.scalar, w0, w0_scales)
+        load_codes(w0, w0_words)
+        load_x(0, 1)
+        load_x(0, 2)
+        load_x(0, 3)
+        nc.gpsimd.dma_start(out=b_rows[0:NT, :], in_=b.rearrange("(j p) -> j p", p=P))
+        nc.gpsimd.dma_start(out=fw_rows[:], in_=fw.rearrange("(g p t) -> p g t", p=P, t=4))
+        load_scales(nc.gpsimd, w1, w1_scales)
+        load_x(1, 0)
+        load_codes(w1, w1_words)
+        for g in range(1, NG):
+            load_x(1, g)
+        nc.scalar.activation(out=warm[:, 4:5], in_=warm[:, 0:1], func=ACT.Tanh)
+        nc.vector.tensor_copy(out=ident_bf[:], in_=ident[:])
+
+        x_grouped = {}
+
+        def turn_x(s, g, h, eng):
+            if h == 0:
+                x_grouped[s, g] = work.tile([P, 4 * PASS], BF16, name="xg", tag="xg", align_bytes=64)
+            words = x_raw[s][g][:].bitcast(F32)
+            bk = bank(eng, [P, 2, 2, P])
+            for e in range(2):
+                for c in range(2):
+                    nc.tensor.transpose(bk[:, e, c, :], words[:, 2 * h + e, c::2], ident[:])
+            dst = x_grouped[s, g][:].bitcast(F32)[:, h * BANK:(h + 1) * BANK]
+            if s == 0:
+                move(eng, dst.rearrange("k (p e c) -> k p e c", e=2, c=2), bk[:].rearrange("k e c p -> k p e c"))
+            else:
+                move(eng, dst.rearrange("k (e p c) -> k e p c", e=2, c=2), bk[:].rearrange("k e c p -> k e p c"))
+
+        def quantise_x(s, g):
+            quantise(xq[s][g], slice(0, PASS), x_grouped[s, g][:])
+
+        def spread_bias():
+            bk = bank(nc.scalar, [P, P], BF16)
+            nc.tensor.transpose(bk[:], b_rows[:], ident_bf[:])
+            nc.scalar.copy(out=b_col[:], in_=bk[:, 0:NT])
+
+        def spread_fw(h, eng):
+            words = fw_rows[:].rearrange("p g t -> p (g t)").bitcast(F32)
+            bk = bank(eng, [P, 4, P])
+            for i in range(4):
+                nc.tensor.transpose(bk[:, i, :], words[:, 4 * h + i:4 * h + i + 1].to_broadcast([P, P]), ident[:])
+            move(eng, fw_all[:].bitcast(F32)[:, h * BANK:(h + 1) * BANK], bk[:].rearrange("q i p -> q (i p)"))
+
+        f_tile, p_rows, p_grouped, v_grouped = {}, {}, {}, {}
+
+        def features(j, g):
+            if g == 0:
+                f_tile[j] = work.tile([P, N], F32, name="f", tag="f")
+            bk = bank(nc.scalar, [P, BANK])
+            mx_pass(bk[:], w0, feat(j), xq[0][g], slice(0, PASS), True, True)
+            nc.scalar.activation(
+                out=f_tile[j][:, g * PASS:(g + 1) * PASS], in_=bk[:], func=ACT.Tanh,
+                bias=b_col[:, j:j + 1], accum_out=sums[:, NG * j + g:NG * j + g + 1],
+            )
+
+        def frame_mean(j):
+            cols = slice(NG * j, NG * (j + 1))
+            nc.scalar.activation(out=parts[:, cols], in_=sums[:, cols], func=ACT.Copy, scale=1.0 / N, accum_out=mean[:, j:j + 1])
+
+        def centre(j, h):
+            if h == 0:
+                p_rows[j] = work.tile([P, N], BF16, name="prow", tag="prow")
+            cols = slice(h * N // 2, (h + 1) * N // 2)
+            nc.vector.scalar_tensor_tensor(
+                out=p_rows[j][:, cols], in0=f_tile[j][:, cols], scalar=mean[:, j:j + 1], in1=fw_all[:, cols],
+                op0=ALU.subtract, op1=ALU.mult,
+            )
+
+        p_bank = {}
+
+        def turn_p(j, h, eng):
+            words = p_rows[j][:].bitcast(F32)
+            p_bank[j, h] = bank(eng, [P, 2, 2, P])
+            for i in range(4):
+                nc.tensor.transpose(p_bank[j, h][:, i // 2, i % 2, :], words[:, feat(4 * h + i)], ident[:])
+
+        def group_p(j, h, eng):
+            if h == 0:
+                p_grouped[j] = work.tile([P, N], BF16, name="pg", tag="pg", align_bytes=64)
+            dst = p_grouped[j][:].bitcast(F32)[:, h * BANK:(h + 1) * BANK]
+            move(eng, dst.rearrange("p (g n u) -> p g n u", g=2, u=2), p_bank[j, h][:].rearrange("p g u n -> p g n u"))
+
+        def quantise_p(j, g):
+            quantise(pq[g], feat(j), p_grouped[j][:, g * PASS:(g + 1) * PASS])
+
+        def linear(j, g, eng):
+            if g == 0:
+                v_grouped[j] = work.tile([P, N], BF16, name="vg", tag="vg", align_bytes=64, bufs=3)
+            bk = bank(eng, [P, 4, P])
+            for t in range(4):
+                mx_pass(bk[:, t, :], xq[1][g], feat(t), w1, feat(j), True, True)
+            dst = v_grouped[j][:, g * PASS:(g + 1) * PASS]
+            move(eng, dst.rearrange("p (n t) -> p n t", t=4), bk[:].rearrange("p t n -> p n t"))
+
+        def quantise_v(j, g):
+            quantise(vq[g], feat(j), v_grouped[j][:, g * PASS:(g + 1) * PASS])
+
+        r_low, r_up, c_bank, up_bank, pl_bank, pl_grouped = {}, {}, {}, {}, {}, {}
+
+        def span(j, h):
+            return h * BANK, min((j + 1) * P, (h + 1) * BANK)
+
+        def cross_passes(j):
+            passes = []
+            for h in range(2):
+                c0, hi = span(j, h)
+                for width in (512, 256, 128):
+                    if c0 + width <= hi:
+                        for i in range(2 * NG):
+                            passes.append((j, h, c0, width, i))
+                        c0 = c0 + width
+            return passes
+
+        def cross(j, h, c0, width, i, eng):
+            lo, hi = span(j, h)
+            if c0 == lo and i == 0:
+                c_bank[j, h] = psum.tile([P, BANK], F32, name="cbank", tag="cbank", bufs=2)
+            stat, mov = (vq, pq) if i < NG else (pq, vq)
+            mx_pass(c_bank[j, h][:, c0 - lo:c0 - lo + width], stat[i % NG], feat(j), mov[i % NG], slice(c0, c0 + width), i == 0, i == 2 * NG - 1)
+
+        def scale_r(j, h, eng):
+            lo, hi = span(j, h)
+            if hi <= lo:
+                return
+            if h == 0:
+                r_low[j] = work.tile([P, (j + 1) * P], F32, name="rlow", tag="rlow", bufs=3)
+            if eng is nc.scalar:
+                eng.activation(out=r_low[j][:, lo:hi], in_=c_bank[j, h][:, 0:hi - lo], func=ACT.Copy, scale=R_SCALE)
+            else:
+                eng.tensor_scalar(out=r_low[j][:, lo:hi], in0=c_bank[j, h][:, 0:hi - lo], scalar1=R_SCALE, scalar2=None, op0=ALU.mult)
+            nc.sync.dma_start(out=out_0[feat(j), lo:hi], in_=r_low[j][:, lo:hi])
+
+        def up_span(j, h):
+            return 4 * h, min(j, 4 * h + 4)
+
+        def turn_r(j, h, eng):
+            lo, hi = up_span(j, h)
+            if hi <= lo:
+                return
+            up_bank[j, h] = bank(eng, [P, 4, P])
+            for i in range(lo, hi):
+                nc.tensor.transpose(up_bank[j, h][:, i - lo, :], r_low[j][:, feat(i)], ident[:])
+
+        def mirror_r(j, h, eng):
+            lo, hi = up_span(j, h)
+            if hi <= lo:
+                return
+            r_up[j, h] = work.tile([P, hi - lo, P], F32, name="rup", tag="rup", bufs=4)
+            move(eng, r_up[j, h][:], up_bank[j, h][:, 0:hi - lo, :])
+            nc.sync.dma_start(out=out_0[lo * P:hi * P, feat(j)].rearrange("(i q) c -> q i c", q=P), in_=r_up[j, h][:])
+
+        def round_low(j, h):
+            lo, hi = span(j, h)
+            if hi <= lo:
+                return
+            dst = r_bf[h][:, j, :].rearrange("m (u p e) -> m u p e", u=2, e=2)[:, :, 0:(hi - lo) // 4, :]
+            nc.vector.tensor_copy(out=dst, in_=r_low[j][:, lo:hi].rearrange("m (p u e) -> m u p e", u=2, e=2))
+
+        def round_up(j, h):
+            lo, hi = up_span(j, h)
+            if hi <= lo:
+                return
+            p0 = 32 * (j % 4)
+            dst = r_bf[j // 4][:, lo:hi, :].rearrange("m i (u p e) -> m u i p e", u=2, e=2)[:, :, :, p0:p0 + 32, :]
+            nc.vector.tensor_copy(out=dst, in_=r_up[j, h][:].rearrange("m i (p u e) -> m u i p e", u=2, e=2))
+
+        def turn_planes(g, m0, n, eng):
+            words = r_bf[g][:].bitcast(F32)
+            pl_bank[g, m0] = bank(eng, [P, 2, 2, P])
+            for i in range(n):
+                for u in range(2):
+                    nc.tensor.transpose(pl_bank[g, m0][:, i, u, :], words[:, m0 + i, feat(u)], ident[:])
+
+        def group_planes(g, m0, n, eng):
+            pl_grouped[g, m0] = work.tile([P, n * PASS], BF16, name="plg", tag="plg", align_bytes=64, bufs=3)
+            dst = pl_grouped[g, m0][:].bitcast(F32).rearrange("p (i m u) -> p i m u", i=n, u=2)
+            move(eng, dst, pl_bank[g, m0][:, 0:n].rearrange("p i u m -> p i m u"))
+
+        def quantise_planes(g, m0, n):
+            cols = slice(m0 * P, (m0 + n) * P)
+            nc.vector.quantize_mx(
+                out=out_codes[g][:, cols].bitcast(FP8X4), scales=out_scales[4 * g:P, cols], in_=pl_grouped[g, m0][:]
+            )
+
+        def store_codes(g, m0, n):
+            cols = slice(m0 * P, (m0 + n) * P)
+            dst = out_1[g].rearrange("p m t -> p (m t)").bitcast(I32)
+            nc.sync.dma_start(out=dst[:, cols], in_=out_codes[g][:, cols].bitcast(I32))
+
+        def store_scales():
+            for q in range(4):
+                nc.sync.dma_start(out=out_2[:, 4 * q:4 * q + 4, :].bitcast(I32), in_=out_scales[32 * q:32 * q + 8, :].bitcast(I32))
+
+        S, V = nc.scalar, nc.vector
+
+        def cross_some(passes, share):
+            total = sum(p[3] for p in passes[0])
+            while passes[1] < len(passes[0]) and sum(p[3] for p in passes[0][:passes[1] + 1]) <= share * total + 1:
+                cross(*passes[0][passes[1]], S)
+                passes[1] = passes[1] + 1
+
+        for g in range(NG):
+            turn_x(0, g, 0, S)
+            turn_x(0, g, 1, V)
+            if g == 0:
+                spread_bias()
+            if g > 1:
+                features(0, g - 2)
+            quantise_x(0, g)
+        spread_fw(0, V)
+        spread_fw(1, V)
+        features(0, 2)
+        features(0, 3)
+        frame_mean(0)
+        for g in range(NG):
+            turn_x(1, g, 0, S if g < XS else V)
+            turn_x(1, g, 1, V)
+            features(1, g)
+            if g in (0, 1):
+                centre(0, g)
+            quantise_x(1, g)
+        frame_mean(1)
+        turn_p(0, 0, V)
+        turn_p(0, 1, V)
+        linear(0, 0, S)
+        group_p(0, 0, V)
+        linear(0, 1, S)
+        group_p(0, 1, V)
+        linear(0, 2, S)
+        linear(0, 3, S)
+        for g in range(NG):
+            quantise_p(0, g)
+            linear(1, g, S)
+        for g in range(NG):
+            quantise_v(0, g)
+
+        for j in range(1, NT + 2):
+            live = j < NT
+            nxt = j + 1 < NT
+            passes = [cross_passes(j - 1) if j - 1 < NT else [], 0]
+            ready = {6: [(0, 0, 2)], 7: [(0, 2, 2)], 8: [(0, 4, 2)]}.get(j, [])
+            if live:
+                centre(j, 0)
+                centre(j, 1)
+            for g in range(NG):
+                if nxt:
+                    features(j + 1, g)
+                cross_some(passes, A1 * (g + 1) / NG)
+            if live:
+                for g in range(NG):
+                    quantise_v(j, g)
+            if j >= 2:
+                turn_r(j - 2, 0, S)
+                turn_r(j - 2, 1, S)
+            for unit in ready:
+                turn_planes(*unit, V)
+            if live:
+                turn_p(j, 0, V)
+                turn_p(j, 1, V)
+            if nxt:
+                frame_mean(j + 1)
+            if j >= 2:
+                mirror_r(j - 2, 0, S)
+                round_low(j - 2, 0)
+                round_low(j - 2, 1)
+            for unit in ready:
+                group_planes(*unit, V)
+            if live:
+                group_p(j, 0, V)
+                group_p(j, 1, V)
+            if j >= 2:
+                mirror_r(j - 2, 1, S)
+            for unit in ready:
+                quantise_planes(*unit)
+                store_codes(*unit)
+            for g in range(NG):
+                if nxt:
+                    linear(j + 1, g, S)
+                cross_some(passes, A1 + (1 - A1) * (g + 1) / NG)
+                if live:
+                    quantise_p(j, g)
+            if j - 1 < NT:
+                scale_r(j - 1, 0, S)
+                scale_r(j - 1, 1, S)
+            if j >= 2:
+                round_up(j - 2, 0)
+                round_up(j - 2, 1)
+        ready = [(1, 0, 2), (1, 2, 2), (1, 4, 2), (1, 6, 2), (0, 6, 2)]
+        for i, unit in enumerate(ready):
+            eng = (S, V)[i % 2]
+            turn_planes(*unit, eng)
+            group_planes(*unit, eng)
+            if i > 0:
+                quantise_planes(*ready[i - 1])
+                store_codes(*ready[i - 1])
+        quantise_planes(*ready[-1])
+        store_codes(*ready[-1])
+        store_scales()

@@ -25,7 +25,18 @@ R_SCALE = 0.5 / math.sqrt(N)
 SB = 6
 VB = 0
 XS = 4
-A1 = 0.3
+BUD = 2
+CB = 2
+J0 = 2
+SRV = 0
+WARM = 0
+B1 = 6
+B2 = 6
+MV = 0
+DD = 5
+LV = 1
+GS = 6
+PB = 4
 
 
 def tile_symmetrisedweightedcrossmoment_kernel(
@@ -79,7 +90,7 @@ def tile_symmetrisedweightedcrossmoment_kernel(
         fw_all = keep.tile([P, N], BF16, name="fw_all")
         sums = keep.tile([P, NT * NG], F32, name="sums")
         parts = keep.tile([P, NT * NG], F32, name="parts")
-        mean = keep.tile([P, NT], F32, name="mean")
+        mean = [keep.tile([P, 1], F32, name="mean%d" % j) for j in range(NT)]
         warm = keep.tile([P, 8], F32, name="warm")
         w0 = mx("w0", F)
         w1 = mx("w1", F)
@@ -109,17 +120,18 @@ def tile_symmetrisedweightedcrossmoment_kernel(
         make_identity(nc, ident[:])
         load_x(0, 0)
         load_scales(nc.scalar, w0, w0_scales)
-        load_codes(w0, w0_words)
         load_x(0, 1)
         load_x(0, 2)
+        load_codes(w0, w0_words)
         load_x(0, 3)
         nc.gpsimd.dma_start(out=b_rows[0:NT, :], in_=b.rearrange("(j p) -> j p", p=P))
         nc.gpsimd.dma_start(out=fw_rows[:], in_=fw.rearrange("(g p t) -> p g t", p=P, t=4))
         load_scales(nc.gpsimd, w1, w1_scales)
         load_x(1, 0)
+        load_x(1, 1)
         load_codes(w1, w1_words)
-        for g in range(1, NG):
-            load_x(1, g)
+        load_x(1, 2)
+        load_x(1, 3)
         nc.scalar.activation(out=warm[:, 4:5], in_=warm[:, 0:1], func=ACT.Tanh)
         nc.vector.tensor_copy(out=ident_bf[:], in_=ident[:])
 
@@ -127,7 +139,7 @@ def tile_symmetrisedweightedcrossmoment_kernel(
 
         def turn_x(s, g, h, eng):
             if h == 0:
-                x_grouped[s, g] = work.tile([P, 4 * PASS], BF16, name="xg", tag="xg", align_bytes=64)
+                x_grouped[s, g] = work.tile([P, 4 * PASS], BF16, name="xg", tag="xg", align_bytes=64, bufs=3)
             words = x_raw[s][g][:].bitcast(F32)
             bk = bank(eng, [P, 2, 2, P])
             for e in range(2):
@@ -168,14 +180,14 @@ def tile_symmetrisedweightedcrossmoment_kernel(
 
         def frame_mean(j):
             cols = slice(NG * j, NG * (j + 1))
-            nc.scalar.activation(out=parts[:, cols], in_=sums[:, cols], func=ACT.Copy, scale=1.0 / N, accum_out=mean[:, j:j + 1])
+            nc.scalar.activation(out=parts[:, cols], in_=sums[:, cols], func=ACT.Copy, scale=1.0 / N, accum_out=mean[j][:])
 
         def centre(j, h):
             if h == 0:
                 p_rows[j] = work.tile([P, N], BF16, name="prow", tag="prow")
             cols = slice(h * N // 2, (h + 1) * N // 2)
             nc.vector.scalar_tensor_tensor(
-                out=p_rows[j][:, cols], in0=f_tile[j][:, cols], scalar=mean[:, j:j + 1], in1=fw_all[:, cols],
+                out=p_rows[j][:, cols], in0=f_tile[j][:, cols], scalar=mean[j][:], in1=fw_all[:, cols],
                 op0=ALU.subtract, op1=ALU.mult,
             )
 
@@ -208,74 +220,69 @@ def tile_symmetrisedweightedcrossmoment_kernel(
         def quantise_v(j, g):
             quantise(vq[g], feat(j), v_grouped[j][:, g * PASS:(g + 1) * PASS])
 
-        r_low, r_up, c_bank, up_bank, pl_bank, pl_grouped = {}, {}, {}, {}, {}, {}
+        r_up, c_bank, up_bank, pl_bank, pl_grouped = {}, {}, {}, {}, {}
+        r_low = [keep.tile([P, (j + 1) * P], F32, name="rlow%d" % j) for j in range(NT)]
 
-        def span(j, h):
-            return h * BANK, min((j + 1) * P, (h + 1) * BANK)
-
-        def cross_passes(j):
+        def cross_passes(chunk):
+            j, lo, hi = chunk
             passes = []
-            for h in range(2):
-                c0, hi = span(j, h)
-                for width in (512, 256, 128):
-                    if c0 + width <= hi:
-                        for i in range(2 * NG):
-                            passes.append((j, h, c0, width, i))
-                        c0 = c0 + width
+            c0 = lo
+            for width in (4, 2, 1):
+                if c0 + width <= hi:
+                    passes.extend([(chunk, c0, width, i) for i in range(2 * NG)])
+                    c0 = c0 + width
             return passes
 
-        def cross(j, h, c0, width, i, eng):
-            lo, hi = span(j, h)
+        def cross(chunk, c0, width, i):
+            j, lo, hi = chunk
             if c0 == lo and i == 0:
-                c_bank[j, h] = psum.tile([P, BANK], F32, name="cbank", tag="cbank", bufs=2)
+                c_bank[chunk] = psum.tile([P, BANK], F32, name="cbank", tag="cbank", bufs=CB)
             stat, mov = (vq, pq) if i < NG else (pq, vq)
-            mx_pass(c_bank[j, h][:, c0 - lo:c0 - lo + width], stat[i % NG], feat(j), mov[i % NG], slice(c0, c0 + width), i == 0, i == 2 * NG - 1)
+            out = c_bank[chunk][:, (c0 - lo) * P:(c0 - lo + width) * P]
+            mx_pass(out, stat[i % NG], feat(j), mov[i % NG], slice(c0 * P, (c0 + width) * P), i == 0, i == 2 * NG - 1)
 
-        def scale_r(j, h, eng):
-            lo, hi = span(j, h)
-            if hi <= lo:
-                return
-            if h == 0:
-                r_low[j] = work.tile([P, (j + 1) * P], F32, name="rlow", tag="rlow", bufs=3)
+        def scale_r(chunk, eng):
+            j, lo, hi = chunk
+            dst = r_low[j][:, lo * P:hi * P]
+            src = c_bank[chunk][:, 0:(hi - lo) * P]
             if eng is nc.scalar:
-                eng.activation(out=r_low[j][:, lo:hi], in_=c_bank[j, h][:, 0:hi - lo], func=ACT.Copy, scale=R_SCALE)
+                eng.activation(out=dst, in_=src, func=ACT.Copy, scale=R_SCALE)
             else:
-                eng.tensor_scalar(out=r_low[j][:, lo:hi], in0=c_bank[j, h][:, 0:hi - lo], scalar1=R_SCALE, scalar2=None, op0=ALU.mult)
-            nc.sync.dma_start(out=out_0[feat(j), lo:hi], in_=r_low[j][:, lo:hi])
+                eng.tensor_scalar(out=dst, in0=src, scalar1=R_SCALE, scalar2=None, op0=ALU.mult)
+            nc.sync.dma_start(out=out_0[feat(j), lo * P:hi * P], in_=dst)
 
-        def up_span(j, h):
-            return 4 * h, min(j, 4 * h + 4)
+        def turn_r(chunk, eng):
+            j, lo, hi = chunk
+            up_bank[chunk] = bank(eng, [P, 4, P])
+            for i in range(lo, min(hi, j)):
+                nc.tensor.transpose(up_bank[chunk][:, i - lo, :], r_low[j][:, feat(i)], ident[:])
 
-        def turn_r(j, h, eng):
-            lo, hi = up_span(j, h)
-            if hi <= lo:
-                return
-            up_bank[j, h] = bank(eng, [P, 4, P])
-            for i in range(lo, hi):
-                nc.tensor.transpose(up_bank[j, h][:, i - lo, :], r_low[j][:, feat(i)], ident[:])
+        def mirror_r(chunk, eng):
+            j, lo, hi = chunk
+            hi = min(hi, j)
+            r_up[chunk] = work.tile([P, hi - lo, P], F32, name="rup", tag="rup", bufs=4)
+            move(eng, r_up[chunk][:], up_bank[chunk][:, 0:hi - lo, :])
+            nc.sync.dma_start(out=out_0[lo * P:hi * P, feat(j)].rearrange("(i q) c -> q i c", q=P), in_=r_up[chunk][:])
 
-        def mirror_r(j, h, eng):
-            lo, hi = up_span(j, h)
-            if hi <= lo:
-                return
-            r_up[j, h] = work.tile([P, hi - lo, P], F32, name="rup", tag="rup", bufs=4)
-            move(eng, r_up[j, h][:], up_bank[j, h][:, 0:hi - lo, :])
-            nc.sync.dma_start(out=out_0[lo * P:hi * P, feat(j)].rearrange("(i q) c -> q i c", q=P), in_=r_up[j, h][:])
+        def round_low(chunk):
+            j, lo, hi = chunk
+            p0 = 32 * (lo % 4)
+            dst = r_bf[lo // 4][:, j, :].rearrange("m (u p e) -> m u p e", u=2, e=2)[:, :, p0:p0 + 32 * (hi - lo), :]
+            nc.vector.tensor_copy(out=dst, in_=r_low[j][:, lo * P:hi * P].rearrange("m (p u e) -> m u p e", u=2, e=2))
 
-        def round_low(j, h):
-            lo, hi = span(j, h)
-            if hi <= lo:
-                return
-            dst = r_bf[h][:, j, :].rearrange("m (u p e) -> m u p e", u=2, e=2)[:, :, 0:(hi - lo) // 4, :]
-            nc.vector.tensor_copy(out=dst, in_=r_low[j][:, lo:hi].rearrange("m (p u e) -> m u p e", u=2, e=2))
-
-        def round_up(j, h):
-            lo, hi = up_span(j, h)
-            if hi <= lo:
-                return
+        def round_up(chunk):
+            j, lo, hi = chunk
+            hi = min(hi, j)
             p0 = 32 * (j % 4)
             dst = r_bf[j // 4][:, lo:hi, :].rearrange("m i (u p e) -> m u i p e", u=2, e=2)[:, :, :, p0:p0 + 32, :]
-            nc.vector.tensor_copy(out=dst, in_=r_up[j, h][:].rearrange("m i (p u e) -> m u i p e", u=2, e=2))
+            nc.vector.tensor_copy(out=dst, in_=r_up[chunk][:].rearrange("m i (p u e) -> m u i p e", u=2, e=2))
+
+        def round_up_from_bank(chunk):
+            j, lo, hi = chunk
+            hi = min(hi, j)
+            p0 = 32 * (j % 4)
+            dst = r_bf[j // 4][:, lo:hi, :].rearrange("m i (u p e) -> m u i p e", u=2, e=2)[:, :, :, p0:p0 + 32, :]
+            nc.vector.tensor_copy(out=dst, in_=up_bank[chunk][:, 0:hi - lo, :].rearrange("m i (p u e) -> m u i p e", u=2, e=2))
 
         def turn_planes(g, m0, n, eng):
             words = r_bf[g][:].bitcast(F32)
@@ -285,7 +292,7 @@ def tile_symmetrisedweightedcrossmoment_kernel(
                     nc.tensor.transpose(pl_bank[g, m0][:, i, u, :], words[:, m0 + i, feat(u)], ident[:])
 
         def group_planes(g, m0, n, eng):
-            pl_grouped[g, m0] = work.tile([P, n * PASS], BF16, name="plg", tag="plg", align_bytes=64, bufs=3)
+            pl_grouped[g, m0] = work.tile([P, n * PASS], BF16, name="plg", tag="plg", align_bytes=64, bufs=PB)
             dst = pl_grouped[g, m0][:].bitcast(F32).rearrange("p (i m u) -> p i m u", i=n, u=2)
             move(eng, dst, pl_bank[g, m0][:, 0:n].rearrange("p i u m -> p i m u"))
 
@@ -306,106 +313,178 @@ def tile_symmetrisedweightedcrossmoment_kernel(
 
         S, V = nc.scalar, nc.vector
 
-        def cross_some(passes, share):
-            total = sum(p[3] for p in passes[0])
-            while passes[1] < len(passes[0]) and sum(p[3] for p in passes[0][:passes[1] + 1]) <= share * total + 1:
-                cross(*passes[0][passes[1]], S)
-                passes[1] = passes[1] + 1
+        queue, scaled, turned = [], [], []
 
-        for g in range(NG):
+        def cross_some(blocks, eng):
+            while queue and blocks > 0:
+                item = queue.pop(0)
+                cross(*item)
+                blocks = blocks - item[2]
+                if not queue or queue[0][0] != item[0]:
+                    scale_r(item[0], eng)
+                    scaled.append(item[0])
+
+        def chunks(j):
+            if j < 4:
+                return [(j, 0, j + 1)]
+            if j < DD:
+                return [(j, 0, 4), (j, 4, j + 1)]
+            return [(j, 0, 4)] + ([(j, 4, j)] if j > 4 else [])
+
+        for g in range(3):
             turn_x(0, g, 0, S)
             turn_x(0, g, 1, V)
-            if g == 0:
-                spread_bias()
-            if g > 1:
-                features(0, g - 2)
             quantise_x(0, g)
+        spread_bias()
+        for g in range(2):
+            features(0, g)
+            features(1, g)
+        turn_x(0, 3, 0, V)
+        turn_x(0, 3, 1, V)
+        quantise_x(0, 3)
         spread_fw(0, V)
         spread_fw(1, V)
         features(0, 2)
         features(0, 3)
+        features(1, 2)
         frame_mean(0)
-        for g in range(NG):
-            turn_x(1, g, 0, S if g < XS else V)
-            turn_x(1, g, 1, V)
-            features(1, g)
-            if g in (0, 1):
-                centre(0, g)
-            quantise_x(1, g)
+        features(1, 3)
+        turn_x(1, 0, 0, S)
         frame_mean(1)
+        turn_x(1, 0, 1, S)
+        centre(0, 0)
+        turn_x(1, 1, 0, S)
+        turn_x(1, 1, 1, S)
+        centre(0, 1)
+        quantise_x(1, 0)
+        turn_x(1, 2, 0, S)
+        turn_x(1, 2, 1, S)
         turn_p(0, 0, V)
         turn_p(0, 1, V)
-        linear(0, 0, S)
+        quantise_x(1, 1)
         group_p(0, 0, V)
-        linear(0, 1, S)
+        turn_x(1, 3, 0, S if XS > 3 else V)
+        turn_x(1, 3, 1, S if XS > 2 else V)
+        quantise_x(1, 2)
         group_p(0, 1, V)
+        linear(0, 0, S)
+        linear(0, 1, S)
+        quantise_x(1, 3)
         linear(0, 2, S)
-        linear(0, 3, S)
         for g in range(NG):
             quantise_p(0, g)
-            linear(1, g, S)
-        for g in range(NG):
-            quantise_v(0, g)
+        features(2, 0)
+        linear(0, 3, S)
+        for g in range(1, NG):
+            features(2, g)
 
-        for j in range(1, NT + 2):
-            live = j < NT
-            nxt = j + 1 < NT
-            passes = [cross_passes(j - 1) if j - 1 < NT else [], 0]
-            ready = {6: [(0, 0, 2)], 7: [(0, 2, 2)], 8: [(0, 4, 2)]}.get(j, [])
-            if live:
-                centre(j, 0)
-                centre(j, 1)
+        planes_at = {6: [(0, 0, 2)], 7: [(0, 2, 2)]}
+        for j in range(1, NT):
+            nxt = j + 2 < NT
+            ready = planes_at.get(j, [])
+            centre(j, 0)
+            if j == 1:
+                for g in range(NG):
+                    quantise_v(0, g)
+            centre(j, 1)
+            todo = [c for c in scaled if c not in turned and c[1] < c[0]][:2] if j >= J0 else []
+            for g in range(NG):
+                linear(j, g, V if g >= NG - LV and j < GS else S)
+                if g == 0 and j + 1 < NT:
+                    frame_mean(j + 1)
+                if g == 0:
+                    for c in chunks(j - 1):
+                        queue.extend(cross_passes(c))
+                cross_some(B1, V if SRV else S)
+            for c in todo:
+                turn_r(c, S)
+            for unit in ready:
+                turn_planes(*unit, S)
+            turn_p(j, 0, V)
+            turn_p(j, 1, V)
+            if j == J0:
+                round_low((0, 0, 1))
+            for c in todo:
+                round_low(c)
+            for i, c in enumerate(todo):
+                mirror_r(c, V if i < MV else S)
+            for unit in ready:
+                group_planes(*unit, S)
+            group_p(j, 0, V if j < GS else S)
+            quantise_v(j, 0)
+            quantise_v(j, 1)
+            group_p(j, 1, V if j < GS else S)
+            quantise_v(j, 2)
+            quantise_v(j, 3)
             for g in range(NG):
                 if nxt:
-                    features(j + 1, g)
-                cross_some(passes, A1 * (g + 1) / NG)
-            if live:
-                for g in range(NG):
-                    quantise_v(j, g)
-            if j >= 2:
-                turn_r(j - 2, 0, S)
-                turn_r(j - 2, 1, S)
-            for unit in ready:
-                turn_planes(*unit, V)
-            if live:
-                turn_p(j, 0, V)
-                turn_p(j, 1, V)
-            if nxt:
-                frame_mean(j + 1)
-            if j >= 2:
-                mirror_r(j - 2, 0, S)
-                round_low(j - 2, 0)
-                round_low(j - 2, 1)
-            for unit in ready:
-                group_planes(*unit, V)
-            if live:
-                group_p(j, 0, V)
-                group_p(j, 1, V)
-            if j >= 2:
-                mirror_r(j - 2, 1, S)
+                    features(j + 2, g)
+                quantise_p(j, g)
+                cross_some(B2, S)
+            for c in todo:
+                round_up(c)
+                turned.append(c)
             for unit in ready:
                 quantise_planes(*unit)
                 store_codes(*unit)
-            for g in range(NG):
-                if nxt:
-                    linear(j + 1, g, S)
-                cross_some(passes, A1 + (1 - A1) * (g + 1) / NG)
-                if live:
-                    quantise_p(j, g)
-            if j - 1 < NT:
-                scale_r(j - 1, 0, S)
-                scale_r(j - 1, 1, S)
-            if j >= 2:
-                round_up(j - 2, 0)
-                round_up(j - 2, 1)
-        ready = [(1, 0, 2), (1, 2, 2), (1, 4, 2), (1, 6, 2), (0, 6, 2)]
-        for i, unit in enumerate(ready):
-            eng = (S, V)[i % 2]
-            turn_planes(*unit, eng)
-            group_planes(*unit, eng)
-            if i > 0:
-                quantise_planes(*ready[i - 1])
-                store_codes(*ready[i - 1])
-        quantise_planes(*ready[-1])
-        store_codes(*ready[-1])
+
+        def whole(chunk, eng):
+            queue.extend(cross_passes(chunk))
+            cross_some(1000, eng)
+
+        cross_some(1000, S)
+        left = [c for c in scaled if c not in turned and c[0] > 0]
+        first, second = (7, 0, 4), (7, 4, 7)
+        whole(first, S)
+        for c in left:
+            if c[1] < c[0]:
+                turn_r(c, S)
+        for c in left:
+            round_low(c)
+            if c[1] < c[0]:
+                mirror_r(c, S)
+        for c in left:
+            if c[1] < c[0]:
+                round_up(c)
+        whole(second, S)
+        round_low(first)
+        turn_r(first, S)
+        turn_planes(0, 4, 2, S)
+        round_up_from_bank(first)
+        group_planes(0, 4, 2, S)
+        mirror_r(first, S)
+        whole((5, 5, 6), V)
+        if DD == 4:
+            whole((4, 4, 5), V)
+        turn_r(second, S)
+        turn_planes(1, 0, 2, S)
+        turn_planes(1, 2, 2, S)
+        turn_planes(0, 6, 2, S)
+        quantise_planes(0, 4, 2)
+        store_codes(0, 4, 2)
+        round_low(second)
+        round_up_from_bank(second)
+        group_planes(1, 0, 2, S)
+        round_low((5, 5, 6))
+        if DD == 4:
+            round_low((4, 4, 5))
+        whole((6, 6, 7), V)
+        group_planes(1, 2, 2, S)
+        whole((7, 7, 8), V)
+        turn_planes(1, 4, 2, S)
+        quantise_planes(1, 0, 2)
+        round_low((6, 6, 7))
+        round_low((7, 7, 8))
+        group_planes(0, 6, 2, S)
+        turn_planes(1, 6, 2, S)
+        quantise_planes(1, 2, 2)
+        store_codes(1, 0, 4)
+        group_planes(1, 4, 2, V)
+        group_planes(1, 6, 2, S)
+        quantise_planes(0, 6, 2)
+        store_codes(0, 6, 2)
+        mirror_r(second, S)
+        quantise_planes(1, 4, 2)
+        quantise_planes(1, 6, 2)
+        store_codes(1, 4, 4)
         store_scales()

@@ -24,10 +24,10 @@ BANK = 512
 R_SCALE = 0.5 / math.sqrt(N)
 SB = 6
 VB = 0
-XS = 4
+XS = 3
 BUD = 2
 CB = 2
-J0 = 2
+J0 = 4
 SRV = 0
 WARM = 0
 B1 = 6
@@ -37,6 +37,12 @@ DD = 5
 LV = 1
 GS = 6
 PB = 4
+Q0 = 0
+W0 = 0
+GQ = 0
+HX = 1
+QJ = 1
+LJ = 8
 
 
 def tile_symmetrisedweightedcrossmoment_kernel(
@@ -86,7 +92,7 @@ def tile_symmetrisedweightedcrossmoment_kernel(
         ident_bf = keep.tile([P, P], BF16, name="ident_bf")
         b_rows = keep.tile([P, P], BF16, name="b_rows")
         b_col = keep.tile([P, NT], F32, name="b_col")
-        fw_rows = keep.tile([P, NG, 4], BF16, name="fw_rows")
+        fw_rows = keep.tile([P, N // P], BF16, name="fw_rows")
         fw_all = keep.tile([P, N], BF16, name="fw_all")
         sums = keep.tile([P, NT * NG], F32, name="sums")
         parts = keep.tile([P, NT * NG], F32, name="parts")
@@ -121,11 +127,14 @@ def tile_symmetrisedweightedcrossmoment_kernel(
         load_x(0, 0)
         load_scales(nc.scalar, w0, w0_scales)
         load_x(0, 1)
+        if W0:
+            load_codes(w0, w0_words)
         load_x(0, 2)
-        load_codes(w0, w0_words)
+        if not W0:
+            load_codes(w0, w0_words)
         load_x(0, 3)
         nc.gpsimd.dma_start(out=b_rows[0:NT, :], in_=b.rearrange("(j p) -> j p", p=P))
-        nc.gpsimd.dma_start(out=fw_rows[:], in_=fw.rearrange("(g p t) -> p g t", p=P, t=4))
+        nc.gpsimd.dma_start(out=fw_rows[:], in_=fw.rearrange("(p i) -> p i", p=P))
         load_scales(nc.gpsimd, w1, w1_scales)
         load_x(1, 0)
         load_x(1, 1)
@@ -134,6 +143,13 @@ def tile_symmetrisedweightedcrossmoment_kernel(
         load_x(1, 3)
         nc.scalar.activation(out=warm[:, 4:5], in_=warm[:, 0:1], func=ACT.Tanh)
         nc.vector.tensor_copy(out=ident_bf[:], in_=ident[:])
+
+        if WARM:
+            zeros = keep.tile([P, BANK], BF16, name="zeros")
+            nc.vector.memset(zeros[:], 0.0)
+            spare = bank(nc.scalar, [P, BANK])
+            for i in range(WARM):
+                nc.tensor.matmul(spare[:], lhsT=zeros[:, 0:P], rhs=zeros[:], start=True, stop=True)
 
         x_grouped = {}
 
@@ -159,18 +175,19 @@ def tile_symmetrisedweightedcrossmoment_kernel(
             nc.tensor.transpose(bk[:], b_rows[:], ident_bf[:])
             nc.scalar.copy(out=b_col[:], in_=bk[:, 0:NT])
 
-        def spread_fw(h, eng):
-            words = fw_rows[:].rearrange("p g t -> p (g t)").bitcast(F32)
+        def spread_fw(u, eng):
+            words = fw_rows[:].bitcast(F32)
             bk = bank(eng, [P, 4, P])
             for i in range(4):
-                nc.tensor.transpose(bk[:, i, :], words[:, 4 * h + i:4 * h + i + 1].to_broadcast([P, P]), ident[:])
-            move(eng, fw_all[:].bitcast(F32)[:, h * BANK:(h + 1) * BANK], bk[:].rearrange("q i p -> q (i p)"))
+                nc.tensor.transpose(bk[:, i, :], words[:, 2 * i + u:2 * i + u + 1].to_broadcast([P, P]), ident[:])
+            dst = fw_all[:].bitcast(F32).rearrange("q (g u r i) -> q g u r i", g=NG, u=2, i=4)[:, :, u, :, :]
+            move(eng, dst, bk[:].rearrange("q i (g r) -> q g r i", g=NG))
 
         f_tile, p_rows, p_grouped, v_grouped = {}, {}, {}, {}
 
         def features(j, g):
             if g == 0:
-                f_tile[j] = work.tile([P, N], F32, name="f", tag="f")
+                f_tile[j] = work.tile([P, N], F32, name="f", tag="f", bufs=3)
             bk = bank(nc.scalar, [P, BANK])
             mx_pass(bk[:], w0, feat(j), xq[0][g], slice(0, PASS), True, True)
             nc.scalar.activation(
@@ -241,7 +258,7 @@ def tile_symmetrisedweightedcrossmoment_kernel(
             out = c_bank[chunk][:, (c0 - lo) * P:(c0 - lo + width) * P]
             mx_pass(out, stat[i % NG], feat(j), mov[i % NG], slice(c0 * P, (c0 + width) * P), i == 0, i == 2 * NG - 1)
 
-        def scale_r(chunk, eng):
+        def scale_r(chunk, eng, queue=nc.sync):
             j, lo, hi = chunk
             dst = r_low[j][:, lo * P:hi * P]
             src = c_bank[chunk][:, 0:(hi - lo) * P]
@@ -249,7 +266,7 @@ def tile_symmetrisedweightedcrossmoment_kernel(
                 eng.activation(out=dst, in_=src, func=ACT.Copy, scale=R_SCALE)
             else:
                 eng.tensor_scalar(out=dst, in0=src, scalar1=R_SCALE, scalar2=None, op0=ALU.mult)
-            nc.sync.dma_start(out=out_0[feat(j), lo * P:hi * P], in_=dst)
+            queue.dma_start(out=out_0[feat(j), lo * P:hi * P], in_=dst)
 
         def turn_r(chunk, eng):
             j, lo, hi = chunk
@@ -283,6 +300,13 @@ def tile_symmetrisedweightedcrossmoment_kernel(
             p0 = 32 * (j % 4)
             dst = r_bf[j // 4][:, lo:hi, :].rearrange("m i (u p e) -> m u i p e", u=2, e=2)[:, :, :, p0:p0 + 32, :]
             nc.vector.tensor_copy(out=dst, in_=up_bank[chunk][:, 0:hi - lo, :].rearrange("m i (p u e) -> m u i p e", u=2, e=2))
+
+        def round_low_from_bank(chunk):
+            j, lo, hi = chunk
+            p0 = 32 * (lo % 4)
+            dst = r_bf[lo // 4][:, j, :].rearrange("m (u p e) -> m u p e", u=2, e=2)[:, :, p0:p0 + 32 * (hi - lo), :]
+            src = c_bank[chunk][:, 0:(hi - lo) * P].rearrange("m (p u e) -> m u p e", u=2, e=2)
+            nc.vector.tensor_scalar(out=dst, in0=src, scalar1=R_SCALE, scalar2=None, op0=ALU.mult)
 
         def turn_planes(g, m0, n, eng):
             words = r_bf[g][:].bitcast(F32)
@@ -335,48 +359,60 @@ def tile_symmetrisedweightedcrossmoment_kernel(
             turn_x(0, g, 0, S)
             turn_x(0, g, 1, V)
             quantise_x(0, g)
-        spread_bias()
-        for g in range(2):
+            if W0 and g == 1:
+                spread_bias()
+                features(0, 0)
+                features(1, 0)
+        if not W0:
+            spread_bias()
+        for g in range(W0, 2):
             features(0, g)
             features(1, g)
         turn_x(0, 3, 0, V)
         turn_x(0, 3, 1, V)
         quantise_x(0, 3)
-        spread_fw(0, V)
+        spread_fw(0, S)
         spread_fw(1, V)
         features(0, 2)
+        if HX:
+            features(1, 2)
+        turn_x(1, 0, 0, V)
+        turn_x(1, 0, 1, V)
         features(0, 3)
-        features(1, 2)
+        if not HX:
+            features(1, 2)
+        if HX == 2:
+            features(1, 3)
         frame_mean(0)
-        features(1, 3)
-        turn_x(1, 0, 0, S)
-        frame_mean(1)
-        turn_x(1, 0, 1, S)
-        centre(0, 0)
-        turn_x(1, 1, 0, S)
-        turn_x(1, 1, 1, S)
-        centre(0, 1)
+        if HX < 2:
+            features(1, 3)
         quantise_x(1, 0)
+        centre(0, 0)
+        centre(0, 1)
+        turn_x(1, 1, 0, S)
+        frame_mean(1)
+        turn_x(1, 1, 1, S)
         turn_x(1, 2, 0, S)
         turn_x(1, 2, 1, S)
-        turn_p(0, 0, V)
-        turn_p(0, 1, V)
         quantise_x(1, 1)
-        group_p(0, 0, V)
+        features(2, 0)
+        features(2, 1)
         turn_x(1, 3, 0, S if XS > 3 else V)
         turn_x(1, 3, 1, S if XS > 2 else V)
+        turn_p(0, 0, V)
+        turn_p(0, 1, V)
         quantise_x(1, 2)
+        group_p(0, 0, V)
         group_p(0, 1, V)
+        quantise_x(1, 3)
         linear(0, 0, S)
         linear(0, 1, S)
-        quantise_x(1, 3)
         linear(0, 2, S)
         for g in range(NG):
             quantise_p(0, g)
-        features(2, 0)
+        features(2, 2)
         linear(0, 3, S)
-        for g in range(1, NG):
-            features(2, g)
+        features(2, 3)
 
         planes_at = {6: [(0, 0, 2)], 7: [(0, 2, 2)]}
         for j in range(1, NT):
@@ -392,7 +428,7 @@ def tile_symmetrisedweightedcrossmoment_kernel(
                 linear(j, g, V if g >= NG - LV and j < GS else S)
                 if g == 0 and j + 1 < NT:
                     frame_mean(j + 1)
-                if g == 0:
+                if g == Q0 and j > QJ:
                     for c in chunks(j - 1):
                         queue.extend(cross_passes(c))
                 cross_some(B1, V if SRV else S)
@@ -416,6 +452,9 @@ def tile_symmetrisedweightedcrossmoment_kernel(
             group_p(j, 1, V if j < GS else S)
             quantise_v(j, 2)
             quantise_v(j, 3)
+            if j <= QJ:
+                for c in chunks(j - 1):
+                    queue.extend(cross_passes(c))
             for g in range(NG):
                 if nxt:
                     features(j + 2, g)
@@ -446,44 +485,47 @@ def tile_symmetrisedweightedcrossmoment_kernel(
         for c in left:
             if c[1] < c[0]:
                 round_up(c)
+        def diagonal(j):
+            for item in cross_passes((j, j, j + 1)):
+                cross(*item)
+
+        side = nc.gpsimd if GQ else nc.sync
         whole(second, S)
         round_low(first)
         turn_r(first, S)
         turn_planes(0, 4, 2, S)
+        turn_planes(0, 6, 2, S)
         round_up_from_bank(first)
         group_planes(0, 4, 2, S)
         mirror_r(first, S)
-        whole((5, 5, 6), V)
-        if DD == 4:
-            whole((4, 4, 5), V)
+        round_low(second)
+        diagonal(5)
         turn_r(second, S)
         turn_planes(1, 0, 2, S)
         turn_planes(1, 2, 2, S)
-        turn_planes(0, 6, 2, S)
-        quantise_planes(0, 4, 2)
-        store_codes(0, 4, 2)
-        round_low(second)
+        group_planes(0, 6, 2, V)
+        round_low_from_bank((5, 5, 6))
         round_up_from_bank(second)
         group_planes(1, 0, 2, S)
-        round_low((5, 5, 6))
-        if DD == 4:
-            round_low((4, 4, 5))
-        whole((6, 6, 7), V)
+        scale_r((5, 5, 6), S, side)
+        quantise_planes(0, 4, 2)
+        quantise_planes(0, 6, 2)
+        store_codes(0, 4, 4)
+        diagonal(6)
+        mirror_r(second, S)
         group_planes(1, 2, 2, S)
-        whole((7, 7, 8), V)
+        diagonal(7)
         turn_planes(1, 4, 2, S)
+        round_low_from_bank((6, 6, 7))
         quantise_planes(1, 0, 2)
-        round_low((6, 6, 7))
-        round_low((7, 7, 8))
-        group_planes(0, 6, 2, S)
+        round_low_from_bank((7, 7, 8))
+        scale_r((6, 6, 7), S, side)
         turn_planes(1, 6, 2, S)
         quantise_planes(1, 2, 2)
         store_codes(1, 0, 4)
         group_planes(1, 4, 2, V)
+        scale_r((7, 7, 8), S)
         group_planes(1, 6, 2, S)
-        quantise_planes(0, 6, 2)
-        store_codes(0, 6, 2)
-        mirror_r(second, S)
         quantise_planes(1, 4, 2)
         quantise_planes(1, 6, 2)
         store_codes(1, 4, 4)

import math
from contextlib import ExitStack

import concourse.mybir as mybir
from concourse.masks import make_identity

N, D, F = 2048, 512, 1024
FLOPS = 2 * N * D * F * 2 + 2 * N * F * F

F32 = mybir.dt.float32
BF16 = mybir.dt.bfloat16
U32 = mybir.dt.uint32
I32 = mybir.dt.int32
U8 = mybir.dt.uint8
FP8X4 = mybir.dt.float8_e4m3fn_x4
ACT = mybir.ActivationFunctionType
ALU = mybir.AluOpType

P = 128
PASS = 512
NG = N // PASS
NT = F // P
BANK = 512
R_SCALE = 0.5 / math.sqrt(N)
SB = 6
VB = 0
XS = 3
BUD = 2
CB = 2
J0 = 4
SRV = 0
WARM = 0
B1 = 6
B2 = 6
MV = 0
DD = 5
LV = 1
GS = 6
PB = 4
Q0 = 0
W0 = 0
GQ = 0
HX = 1
QJ = 1
LJ = 8


def tile_symmetrisedweightedcrossmoment_kernel(
    tc, x0, x1, w0_words, w0_scales, b, w1_words, w1_scales, fw, out_0, out_1, out_2
):
    nc = tc.nc
    with ExitStack() as ctx:
        keep = ctx.enter_context(tc.tile_pool(name="keep", bufs=1))
        work = ctx.enter_context(tc.tile_pool(name="work", bufs=2))
        psum = ctx.enter_context(tc.psum_pool(name="psum", bufs=1))
        ctx.enter_context(tc.manual_schedule())

        def bank(reader, shape, dtype=F32):
            if VB == 0 or reader is nc.scalar:
                return psum.tile(shape, dtype, name="sbank", tag="sbank", bufs=SB)
            return psum.tile(shape, dtype, name="vbank", tag="vbank", bufs=VB)

        def move(eng, out, in_):
            if eng is nc.scalar:
                eng.copy(out=out, in_=in_)
            else:
                eng.tensor_copy(out=out, in_=in_)

        def mx(name, width):
            codes = keep.tile([P, width], U32, name=name + "_codes", align_bytes=64)
            scales = keep.tile([P, width], U8, name=name + "_scales", align_bytes=64)
            return codes, scales

        def quantise(dst, cols, src):
            nc.vector.quantize_mx(out=dst[0][:, cols].bitcast(FP8X4), scales=dst[1][:, cols], in_=src)

        def mx_pass(out, stat, stat_cols, mov, mov_cols, start, stop):
            nc.tensor.matmul_mx(
                out=out,
                lhsT=stat[0][:, stat_cols].bitcast(FP8X4),
                lhsT_scale=stat[1][:, stat_cols],
                rhs=mov[0][:, mov_cols].bitcast(FP8X4),
                rhs_scale=mov[1][:, mov_cols],
                start=start,
                stop=stop,
            )

        def feat(j):
            return slice(j * P, (j + 1) * P)

        ident = keep.tile([P, P], F32, name="ident")
        ident_bf = keep.tile([P, P], BF16, name="ident_bf")
        b_rows = keep.tile([P, P], BF16, name="b_rows")
        b_col = keep.tile([P, NT], F32, name="b_col")
        fw_rows = keep.tile([P, N // P], BF16, name="fw_rows")
        fw_all = keep.tile([P, N], BF16, name="fw_all")
        sums = keep.tile([P, NT * NG], F32, name="sums")
        parts = keep.tile([P, NT * NG], F32, name="parts")
        mean = [keep.tile([P, 1], F32, name="mean%d" % j) for j in range(NT)]
        warm = keep.tile([P, 8], F32, name="warm")
        w0 = mx("w0", F)
        w1 = mx("w1", F)
        xq = [[mx("x%d_%d" % (s, g), PASS) for g in range(NG)] for s in range(2)]
        pq = [mx("p%d" % g, F) for g in range(NG)]
        vq = [mx("v%d" % g, F) for g in range(NG)]
        x_raw = [[keep.tile([P, 4, D], BF16, name="xraw%d_%d" % (s, g)) for g in range(NG)] for s in range(2)]
        r_bf = [keep.tile([P, NT, PASS], BF16, name="rbf%d" % g) for g in range(2)]
        out_codes = [keep.tile([P, F], U32, name="ocodes%d" % g, align_bytes=64) for g in range(2)]
        out_scales = keep.tile([P, F], U8, name="oscales", align_bytes=64)

        def load_x(s, g):
            src = (x0, x1)[s][g * PASS:(g + 1) * PASS, :]
            nc.sync.dma_start(out=x_raw[s][g][:], in_=src.rearrange("(p t) d -> p t d", t=4))

        def load_codes(w, words):
            nc.sync.dma_start(out=w[0][:].bitcast(I32), in_=words[0].rearrange("p n t -> p (n t)").bitcast(I32))

        def load_scales(queue, w, scales):
            for q in range(4):
                queue.dma_start(out=w[1][32 * q:32 * q + 4, :].bitcast(I32), in_=scales[0, 4 * q:4 * q + 4, :].bitcast(I32))

        nc.vector.memset(w0[1][:].bitcast(I32), 0)
        nc.vector.memset(w1[1][:].bitcast(I32), 0)
        nc.vector.memset(b_rows[:], 0.0)
        nc.vector.memset(warm[:], 0.0)
        make_identity(nc, ident[:])
        load_x(0, 0)
        load_scales(nc.scalar, w0, w0_scales)
        load_x(0, 1)
        if W0:
            load_codes(w0, w0_words)
        load_x(0, 2)
        if not W0:
            load_codes(w0, w0_words)
        load_x(0, 3)
        nc.gpsimd.dma_start(out=b_rows[0:NT, :], in_=b.rearrange("(j p) -> j p", p=P))
        nc.gpsimd.dma_start(out=fw_rows[:], in_=fw.rearrange("(p i) -> p i", p=P))
        load_scales(nc.gpsimd, w1, w1_scales)
        load_x(1, 0)
        load_x(1, 1)
        load_codes(w1, w1_words)
        load_x(1, 2)
        load_x(1, 3)
        nc.scalar.activation(out=warm[:, 4:5], in_=warm[:, 0:1], func=ACT.Tanh)
        nc.vector.tensor_copy(out=ident_bf[:], in_=ident[:])

        if WARM:
            zeros = keep.tile([P, BANK], BF16, name="zeros")
            nc.vector.memset(zeros[:], 0.0)
            spare = bank(nc.scalar, [P, BANK])
            for i in range(WARM):
                nc.tensor.matmul(spare[:], lhsT=zeros[:, 0:P], rhs=zeros[:], start=True, stop=True)

        x_grouped = {}

        def turn_x(s, g, h, eng):
            if h == 0:
                x_grouped[s, g] = work.tile([P, 4 * PASS], BF16, name="xg", tag="xg", align_bytes=64, bufs=3)
            words = x_raw[s][g][:].bitcast(F32)
            bk = bank(eng, [P, 2, 2, P])
            for e in range(2):
                for c in range(2):
                    nc.tensor.transpose(bk[:, e, c, :], words[:, 2 * h + e, c::2], ident[:])
            dst = x_grouped[s, g][:].bitcast(F32)[:, h * BANK:(h + 1) * BANK]
            if s == 0:
                move(eng, dst.rearrange("k (p e c) -> k p e c", e=2, c=2), bk[:].rearrange("k e c p -> k p e c"))
            else:
                move(eng, dst.rearrange("k (e p c) -> k e p c", e=2, c=2), bk[:].rearrange("k e c p -> k e p c"))

        def quantise_x(s, g):
            quantise(xq[s][g], slice(0, PASS), x_grouped[s, g][:])

        def spread_bias():
            bk = bank(nc.scalar, [P, P], BF16)
            nc.tensor.transpose(bk[:], b_rows[:], ident_bf[:])
            nc.scalar.copy(out=b_col[:], in_=bk[:, 0:NT])

        def spread_fw(u, eng):
            words = fw_rows[:].bitcast(F32)
            bk = bank(eng, [P, 4, P])
            for i in range(4):
                nc.tensor.transpose(bk[:, i, :], words[:, 2 * i + u:2 * i + u + 1].to_broadcast([P, P]), ident[:])
            dst = fw_all[:].bitcast(F32).rearrange("q (g u r i) -> q g u r i", g=NG, u=2, i=4)[:, :, u, :, :]
            move(eng, dst, bk[:].rearrange("q i (g r) -> q g r i", g=NG))

        f_tile, p_rows, p_grouped, v_grouped = {}, {}, {}, {}

        def features(j, g):
            if g == 0:
                f_tile[j] = work.tile([P, N], F32, name="f", tag="f", bufs=3)
            bk = bank(nc.scalar, [P, BANK])
            mx_pass(bk[:], w0, feat(j), xq[0][g], slice(0, PASS), True, True)
            nc.scalar.activation(
                out=f_tile[j][:, g * PASS:(g + 1) * PASS], in_=bk[:], func=ACT.Tanh,
                bias=b_col[:, j:j + 1], accum_out=sums[:, NG * j + g:NG * j + g + 1],
            )

        def frame_mean(j):
            cols = slice(NG * j, NG * (j + 1))
            nc.scalar.activation(out=parts[:, cols], in_=sums[:, cols], func=ACT.Copy, scale=1.0 / N, accum_out=mean[j][:])

        def centre(j, h):
            if h == 0:
                p_rows[j] = work.tile([P, N], BF16, name="prow", tag="prow")
            cols = slice(h * N // 2, (h + 1) * N // 2)
            nc.vector.scalar_tensor_tensor(
                out=p_rows[j][:, cols], in0=f_tile[j][:, cols], scalar=mean[j][:], in1=fw_all[:, cols],
                op0=ALU.subtract, op1=ALU.mult,
            )

        p_bank = {}

        def turn_p(j, h, eng):
            words = p_rows[j][:].bitcast(F32)
            p_bank[j, h] = bank(eng, [P, 2, 2, P])
            for i in range(4):
                nc.tensor.transpose(p_bank[j, h][:, i // 2, i % 2, :], words[:, feat(4 * h + i)], ident[:])

        def group_p(j, h, eng):
            if h == 0:
                p_grouped[j] = work.tile([P, N], BF16, name="pg", tag="pg", align_bytes=64)
            dst = p_grouped[j][:].bitcast(F32)[:, h * BANK:(h + 1) * BANK]
            move(eng, dst.rearrange("p (g n u) -> p g n u", g=2, u=2), p_bank[j, h][:].rearrange("p g u n -> p g n u"))

        def quantise_p(j, g):
            quantise(pq[g], feat(j), p_grouped[j][:, g * PASS:(g + 1) * PASS])

        def linear(j, g, eng):
            if g == 0:
                v_grouped[j] = work.tile([P, N], BF16, name="vg", tag="vg", align_bytes=64, bufs=3)
            bk = bank(eng, [P, 4, P])
            for t in range(4):
                mx_pass(bk[:, t, :], xq[1][g], feat(t), w1, feat(j), True, True)
            dst = v_grouped[j][:, g * PASS:(g + 1) * PASS]
            move(eng, dst.rearrange("p (n t) -> p n t", t=4), bk[:].rearrange("p t n -> p n t"))

        def quantise_v(j, g):
            quantise(vq[g], feat(j), v_grouped[j][:, g * PASS:(g + 1) * PASS])

        r_up, c_bank, up_bank, pl_bank, pl_grouped = {}, {}, {}, {}, {}
        r_low = [keep.tile([P, (j + 1) * P], F32, name="rlow%d" % j) for j in range(NT)]

        def cross_passes(chunk):
            j, lo, hi = chunk
            passes = []
            c0 = lo
            for width in (4, 2, 1):
                if c0 + width <= hi:
                    passes.extend([(chunk, c0, width, i) for i in range(2 * NG)])
                    c0 = c0 + width
            return passes

        def cross(chunk, c0, width, i):
            j, lo, hi = chunk
            if c0 == lo and i == 0:
                c_bank[chunk] = psum.tile([P, BANK], F32, name="cbank", tag="cbank", bufs=CB)
            stat, mov = (vq, pq) if i < NG else (pq, vq)
            out = c_bank[chunk][:, (c0 - lo) * P:(c0 - lo + width) * P]
            mx_pass(out, stat[i % NG], feat(j), mov[i % NG], slice(c0 * P, (c0 + width) * P), i == 0, i == 2 * NG - 1)

        def scale_r(chunk, eng, queue=nc.sync):
            j, lo, hi = chunk
            dst = r_low[j][:, lo * P:hi * P]
            src = c_bank[chunk][:, 0:(hi - lo) * P]
            if eng is nc.scalar:
                eng.activation(out=dst, in_=src, func=ACT.Copy, scale=R_SCALE)
            else:
                eng.tensor_scalar(out=dst, in0=src, scalar1=R_SCALE, scalar2=None, op0=ALU.mult)
            queue.dma_start(out=out_0[feat(j), lo * P:hi * P], in_=dst)

        def turn_r(chunk, eng):
            j, lo, hi = chunk
            up_bank[chunk] = bank(eng, [P, 4, P])
            for i in range(lo, min(hi, j)):
                nc.tensor.transpose(up_bank[chunk][:, i - lo, :], r_low[j][:, feat(i)], ident[:])

        def mirror_r(chunk, eng):
            j, lo, hi = chunk
            hi = min(hi, j)
            r_up[chunk] = work.tile([P, hi - lo, P], F32, name="rup", tag="rup", bufs=4)
            move(eng, r_up[chunk][:], up_bank[chunk][:, 0:hi - lo, :])
            nc.sync.dma_start(out=out_0[lo * P:hi * P, feat(j)].rearrange("(i q) c -> q i c", q=P), in_=r_up[chunk][:])

        def round_low(chunk):
            j, lo, hi = chunk
            p0 = 32 * (lo % 4)
            dst = r_bf[lo // 4][:, j, :].rearrange("m (u p e) -> m u p e", u=2, e=2)[:, :, p0:p0 + 32 * (hi - lo), :]
            nc.vector.tensor_copy(out=dst, in_=r_low[j][:, lo * P:hi * P].rearrange("m (p u e) -> m u p e", u=2, e=2))

        def round_up(chunk):
            j, lo, hi = chunk
            hi = min(hi, j)
            p0 = 32 * (j % 4)
            dst = r_bf[j // 4][:, lo:hi, :].rearrange("m i (u p e) -> m u i p e", u=2, e=2)[:, :, :, p0:p0 + 32, :]
            nc.vector.tensor_copy(out=dst, in_=r_up[chunk][:].rearrange("m i (p u e) -> m u i p e", u=2, e=2))

        def round_up_from_bank(chunk):
            j, lo, hi = chunk
            hi = min(hi, j)
            p0 = 32 * (j % 4)
            dst = r_bf[j // 4][:, lo:hi, :].rearrange("m i (u p e) -> m u i p e", u=2, e=2)[:, :, :, p0:p0 + 32, :]
            nc.vector.tensor_copy(out=dst, in_=up_bank[chunk][:, 0:hi - lo, :].rearrange("m i (p u e) -> m u i p e", u=2, e=2))

        def round_low_from_bank(chunk):
            j, lo, hi = chunk
            p0 = 32 * (lo % 4)
            dst = r_bf[lo // 4][:, j, :].rearrange("m (u p e) -> m u p e", u=2, e=2)[:, :, p0:p0 + 32 * (hi - lo), :]
            src = c_bank[chunk][:, 0:(hi - lo) * P].rearrange("m (p u e) -> m u p e", u=2, e=2)
            nc.vector.tensor_scalar(out=dst, in0=src, scalar1=R_SCALE, scalar2=None, op0=ALU.mult)

        def turn_planes(g, m0, n, eng):
            words = r_bf[g][:].bitcast(F32)
            pl_bank[g, m0] = bank(eng, [P, 2, 2, P])
            for i in range(n):
                for u in range(2):
                    nc.tensor.transpose(pl_bank[g, m0][:, i, u, :], words[:, m0 + i, feat(u)], ident[:])

        def group_planes(g, m0, n, eng):
            pl_grouped[g, m0] = work.tile([P, n * PASS], BF16, name="plg", tag="plg", align_bytes=64, bufs=PB)
            dst = pl_grouped[g, m0][:].bitcast(F32).rearrange("p (i m u) -> p i m u", i=n, u=2)
            move(eng, dst, pl_bank[g, m0][:, 0:n].rearrange("p i u m -> p i m u"))

        def quantise_planes(g, m0, n):
            cols = slice(m0 * P, (m0 + n) * P)
            nc.vector.quantize_mx(
                out=out_codes[g][:, cols].bitcast(FP8X4), scales=out_scales[4 * g:P, cols], in_=pl_grouped[g, m0][:]
            )

        def store_codes(g, m0, n):
            cols = slice(m0 * P, (m0 + n) * P)
            dst = out_1[g].rearrange("p m t -> p (m t)").bitcast(I32)
            nc.sync.dma_start(out=dst[:, cols], in_=out_codes[g][:, cols].bitcast(I32))

        def store_scales():
            for q in range(4):
                nc.sync.dma_start(out=out_2[:, 4 * q:4 * q + 4, :].bitcast(I32), in_=out_scales[32 * q:32 * q + 8, :].bitcast(I32))

        S, V = nc.scalar, nc.vector

        queue, scaled, turned = [], [], []

        def cross_some(blocks, eng):
            while queue and blocks > 0:
                item = queue.pop(0)
                cross(*item)
                blocks = blocks - item[2]
                if not queue or queue[0][0] != item[0]:
                    scale_r(item[0], eng)
                    scaled.append(item[0])

        def chunks(j):
            if j < 4:
                return [(j, 0, j + 1)]
            if j < DD:
                return [(j, 0, 4), (j, 4, j + 1)]
            return [(j, 0, 4)] + ([(j, 4, j)] if j > 4 else [])

        for g in range(3):
            turn_x(0, g, 0, S)
            turn_x(0, g, 1, V)
            quantise_x(0, g)
            if W0 and g == 1:
                spread_bias()
                features(0, 0)
                features(1, 0)
        if not W0:
            spread_bias()
        for g in range(W0, 2):
            features(0, g)
            features(1, g)
        turn_x(0, 3, 0, V)
        turn_x(0, 3, 1, V)
        quantise_x(0, 3)
        spread_fw(0, S)
        spread_fw(1, V)
        features(0, 2)
        if HX:
            features(1, 2)
        turn_x(1, 0, 0, V)
        turn_x(1, 0, 1, V)
        features(0, 3)
        if not HX:
            features(1, 2)
        if HX == 2:
            features(1, 3)
        frame_mean(0)
        if HX < 2:
            features(1, 3)
        quantise_x(1, 0)
        centre(0, 0)
        centre(0, 1)
        turn_x(1, 1, 0, S)
        frame_mean(1)
        turn_x(1, 1, 1, S)
        turn_x(1, 2, 0, S)
        turn_x(1, 2, 1, S)
        quantise_x(1, 1)
        features(2, 0)
        features(2, 1)
        turn_x(1, 3, 0, S if XS > 3 else V)
        turn_x(1, 3, 1, S if XS > 2 else V)
        turn_p(0, 0, V)
        turn_p(0, 1, V)
        quantise_x(1, 2)
        group_p(0, 0, V)
        group_p(0, 1, V)
        quantise_x(1, 3)
        linear(0, 0, S)
        linear(0, 1, S)
        linear(0, 2, S)
        for g in range(NG):
            quantise_p(0, g)
        features(2, 2)
        linear(0, 3, S)
        features(2, 3)

        planes_at = {6: [(0, 0, 2)], 7: [(0, 2, 2)]}
        for j in range(1, NT):
            nxt = j + 2 < NT
            ready = planes_at.get(j, [])
            centre(j, 0)
            if j == 1:
                for g in range(NG):
                    quantise_v(0, g)
            centre(j, 1)
            todo = [c for c in scaled if c not in turned and c[1] < c[0]][:2] if j >= J0 else []
            for g in range(NG):
                linear(j, g, V if g >= NG - LV and j < GS else S)
                if g == 0 and j + 1 < NT:
                    frame_mean(j + 1)
                if g == Q0 and j > QJ:
                    for c in chunks(j - 1):
                        queue.extend(cross_passes(c))
                cross_some(B1, V if SRV else S)
            for c in todo:
                turn_r(c, S)
            for unit in ready:
                turn_planes(*unit, S)
            turn_p(j, 0, V)
            turn_p(j, 1, V)
            if j == J0:
                round_low((0, 0, 1))
            for c in todo:
                round_low(c)
            for i, c in enumerate(todo):
                mirror_r(c, V if i < MV else S)
            for unit in ready:
                group_planes(*unit, S)
            group_p(j, 0, V if j < GS else S)
            quantise_v(j, 0)
            quantise_v(j, 1)
            group_p(j, 1, V if j < GS else S)
            quantise_v(j, 2)
            quantise_v(j, 3)
            if j <= QJ:
                for c in chunks(j - 1):
                    queue.extend(cross_passes(c))
            for g in range(NG):
                if nxt:
                    features(j + 2, g)
                quantise_p(j, g)
                cross_some(B2, S)
            for c in todo:
                round_up(c)
                turned.append(c)
            for unit in ready:
                quantise_planes(*unit)
                store_codes(*unit)

        def whole(chunk, eng):
            queue.extend(cross_passes(chunk))
            cross_some(1000, eng)

        cross_some(1000, S)
        left = [c for c in scaled if c not in turned and c[0] > 0]
        first, second = (7, 0, 4), (7, 4, 7)
        whole(first, S)
        for c in left:
            if c[1] < c[0]:
                turn_r(c, S)
        for c in left:
            round_low(c)
            if c[1] < c[0]:
                mirror_r(c, S)
        for c in left:
            if c[1] < c[0]:
                round_up(c)
        def diagonal(j):
            for item in cross_passes((j, j, j + 1)):
                cross(*item)

        side = nc.gpsimd if GQ else nc.sync
        whole(second, S)
        round_low(first)
        turn_r(first, S)
        turn_planes(0, 4, 2, S)
        turn_planes(0, 6, 2, S)
        round_up_from_bank(first)
        group_planes(0, 4, 2, S)
        mirror_r(first, S)
        round_low(second)
        diagonal(5)
        turn_r(second, S)
        turn_planes(1, 0, 2, S)
        turn_planes(1, 2, 2, S)
        group_planes(0, 6, 2, V)
        round_low_from_bank((5, 5, 6))
        round_up_from_bank(second)
        group_planes(1, 0, 2, S)
        scale_r((5, 5, 6), S, side)
        quantise_planes(0, 4, 2)
        quantise_planes(0, 6, 2)
        store_codes(0, 4, 4)
        diagonal(6)
        mirror_r(second, S)
        group_planes(1, 2, 2, S)
        diagonal(7)
        turn_planes(1, 4, 2, S)
        round_low_from_bank((6, 6, 7))
        quantise_planes(1, 0, 2)
        round_low_from_bank((7, 7, 8))
        scale_r((6, 6, 7), S, side)
        turn_planes(1, 6, 2, S)
        quantise_planes(1, 2, 2)
        store_codes(1, 0, 4)
        group_planes(1, 4, 2, V)
        scale_r((7, 7, 8), S)
        group_planes(1, 6, 2, S)
        quantise_planes(1, 4, 2)
        quantise_planes(1, 6, 2)
        store_codes(1, 4, 4)
        store_scales()
